import numpy as np
import ml_dtypes


def mxq(x, axis, fmt="e4m3"):
    dtype, down = {"e4m3": (ml_dtypes.float8_e4m3fn, 7), "e5m2": (ml_dtypes.float8_e5m2, 14)}[fmt]
    v = np.moveaxis(np.asarray(x, np.float32).astype(ml_dtypes.bfloat16).astype(np.float64), axis, -1)
    blocks = v.reshape(v.shape[:-1] + (-1, 32))
    amax = np.abs(blocks).max(-1, keepdims=True)
    byte = np.maximum(np.where(amax > 0, np.frexp(amax)[1] - 1 + 127, 0) - down, 1)
    scale = np.exp2(byte - 127.0)
    codes = (blocks / scale).astype(np.float32).astype(dtype).astype(np.float64)
    return np.moveaxis((codes * scale).reshape(v.shape), -1, axis)


WIDE = False


def mx_kscale(k):
    if not WIDE:
        return np.ones(k)
    levels = np.array([30, -30])
    if k % 512:
        return np.exp2(np.random.permutation(np.resize(levels, k // 32))).repeat(32)
    a = np.empty((k // 512, 16))
    for p in range(k // 512):
        a[p, :8] = np.random.permutation(np.resize(levels, 8))
        for g in range(8):
            far = levels[np.abs(levels - a[p, g]) >= 10]
            a[p, g + 8] = far[np.random.randint(len(far))]
    return np.exp2(a.ravel()).repeat(32)


def f64(x):
    return np.asarray(x).astype(np.float64)


def striped(idx):
    return np.tile(np.asarray(idx).reshape(-1, 16).T, (8, 1)).astype(np.uint16)


def unstriped(offs):
    return offs[:16].T.reshape(-1).astype(np.int64)


E2M1 = np.array([0.0, 0.5, 1.0, 1.5, 2.0, 3.0, 4.0, 6.0, -0.0, -0.5, -1.0, -1.5, -2.0, -3.0, -4.0, -6.0])


def pack_weight(w, fmt):
    k, n = w.shape
    w = f64(np.asarray(w, np.float32).astype(ml_dtypes.bfloat16)).reshape(k // 32, 32, n)
    amax = np.abs(w).max(1)
    if fmt in ("e4m3", "e5m2"):
        byte = np.frexp(amax)[1] - 1 + 127 - (7 if fmt == "e4m3" else 14)
    else:
        mant, ex = np.frexp(amax / 6.0)
        byte = np.where(mant > 0.5, ex, ex - 1) + 127
    byte = np.clip(np.where(amax > 0, byte, 1), 1, 254)
    scaled = (w * np.exp2(127.0 - byte)[:, None, :]).reshape(k, n).astype(np.float32)
    by_word = np.ascontiguousarray(scaled.reshape(k // 512, 128, 4, n).transpose(0, 1, 3, 2))
    if fmt in ("e4m3", "e5m2"):
        words = by_word.astype(ml_dtypes.float8_e4m3fn if fmt == "e4m3" else ml_dtypes.float8_e5m2).view(np.uint8)
    else:
        c = by_word.astype(ml_dtypes.float4_e2m1fn).view(np.uint8) & 0xF
        words = (c[..., 0::2] | (c[..., 1::2] << 4)).reshape(k // 512, 128, 2 * n)
    return np.ascontiguousarray(words), np.ascontiguousarray(byte.astype(np.uint8).reshape(k // 512, 16, n))


def unpack_weight(words, scales, fmt):
    g, _, n = scales.shape
    words = np.ascontiguousarray(words).reshape(g, 128, n, -1)
    if fmt in ("e4m3", "e5m2"):
        vals = words.view(ml_dtypes.float8_e4m3fn if fmt == "e4m3" else ml_dtypes.float8_e5m2).astype(np.float64)
    else:
        nib = np.empty((g, 128, n, 4), np.uint8)
        nib[..., 0::2] = words & 0xF
        nib[..., 1::2] = words >> 4
        vals = E2M1[nib]
    vals = vals * np.repeat(np.exp2(scales.astype(np.float64) - 127.0), 8, axis=1)[..., None]
    return vals.transpose(0, 1, 3, 2).reshape(g * 512, n)


K, T, J, R, F, Z, O, U, D, N, E = 512, 1024, 256, 512, 512, 1024, 128, 128, 256, 256, 512


def setup_inputs():
    n = np.random.standard_normal
    idx = np.random.permutation(T)[:J]
    idx2 = np.random.permutation(Z)[:J]
    idx3 = np.random.permutation(J)[:O]
    idx4 = np.random.permutation(J)[:U]
    idx5 = np.random.permutation(T)[:D]
    idx6 = np.random.permutation(E)[:D]
    idx7 = np.random.permutation(E)[:D]
    fk = mx_kscale(K)
    ff = mx_kscale(F)
    fr = mx_kscale(R)
    xtp = pack_weight(n((K, T)) / fk[:, None], "e2m1")
    xop = pack_weight(n((F, Z)) / ff[:, None], "e4m3")
    wp = pack_weight(n((K, R)) * 1 / np.sqrt(K) * fk[:, None] * fr, "e4m3")
    w2p = pack_weight(n((K, R)) * 1 / np.sqrt(K) * fk[:, None], "e5m2")
    w0p = pack_weight(n((F, R)) * 1 / np.sqrt(F) * ff[:, None], "e5m2")
    wbp = pack_weight(n((R, N)) * 1 / np.sqrt(R) / fr[:, None], "e2m1")
    wsp = pack_weight(n((K, N)) * 1 / np.sqrt(K) * fk[:, None], "e4m3")
    return {
        "xt_words": xtp[0],
        "xt_scales": xtp[1],
        "xo_words": xop[0],
        "xo_scales": xop[1],
        "w_words": wp[0],
        "w_scales": wp[1],
        "w2_words": w2p[0],
        "w2_scales": w2p[1],
        "w0_words": w0p[0],
        "w0_scales": w0p[1],
        "wb_words": wbp[0],
        "wb_scales": wbp[1],
        "ws_words": wsp[0],
        "ws_scales": wsp[1],
        "offs": striped(idx),
        "offs2": striped(idx2),
        "offs3": striped(idx3),
        "offs4": striped(idx4),
        "offs5": striped(idx5),
        "offs6": striped(idx6),
        "offs7": striped(idx7),
    }


def reference(xt_words, xt_scales, xo_words, xo_scales, w_words, w_scales, w2_words, w2_scales, w0_words, w0_scales, wb_words, wb_scales, ws_words, ws_scales, offs, offs2, offs3, offs4, offs5, offs6, offs7):
    idx = unstriped(offs)
    idx2 = unstriped(offs2)
    idx3 = unstriped(offs3)
    idx4 = unstriped(offs4)
    idx5 = unstriped(offs5)
    idx6 = unstriped(offs6)
    idx7 = unstriped(offs7)
    xtu = unpack_weight(xt_words, xt_scales, "e2m1")
    xou = unpack_weight(xo_words, xo_scales, "e4m3")
    wu = unpack_weight(w_words, w_scales, "e4m3")
    w2u = unpack_weight(w2_words, w2_scales, "e5m2")
    w0u = unpack_weight(w0_words, w0_scales, "e5m2")
    wbu = unpack_weight(wb_words, wb_scales, "e2m1")
    wsu = unpack_weight(ws_words, ws_scales, "e4m3")
    xtidxg = xtu[:, idx]
    a = wu.T @ xtidxg
    xoidx2g = xou[:, idx2]
    b = w2u.T @ xtidxg + w0u.T @ xoidx2g
    lb = b[:, 0:1]
    la = a[:, 0:1]
    h1 = a[:, idx3] * lb
    h2 = b[:, idx4] * la
    hid = np.concatenate([h1, h2], axis=1)
    hidq = mxq(hid, 0, "e5m2")
    xtidx5g = xtu[:, idx5]
    p = wbu.T @ hidq + wsu.T @ xtidx5g
    pa = np.zeros((N, E))
    pa[:, idx6] = p
    pb = np.zeros((N, E))
    pb[:, idx7] = p
    y = pa + pb
    return y

@@ -1,0 +1,217 @@
+from contextlib import ExitStack
+
+import concourse.mybir as mybir
+
+K, T, J, R, F, Z, O, U, D, N, E = 512, 1024, 256, 512, 512, 1024, 128, 128, 256, 256, 512
+FLOPS = 2 * (3 * K * R * J + 2 * R * N * D)
+
+F32 = mybir.dt.float32
+BF16 = mybir.dt.bfloat16
+I32 = mybir.dt.int32
+U32 = mybir.dt.uint32
+U16 = mybir.dt.uint16
+U8 = mybir.dt.uint8
+E4M3 = mybir.dt.float8_e4m3fn_x4
+E5M2 = mybir.dt.float8_e5m2_x4
+E2M1 = mybir.dt.float4_e2m1fn_x4
+COPY = mybir.ActivationFunctionType.Copy
+ADD = mybir.AluOpType.add
+
+P = 128
+PACK = 4
+QUADS = 4
+LANES = 16
+HALF = D // 2
+
+
+def tile_list_sidebyside_leaned_further_pagetwice_kernel(
+    tc, xt_words, xt_scales, xo_words, xo_scales, w_words, w_scales, w2_words, w2_scales, w0_words, w0_scales,
+    wb_words, wb_scales, ws_words, ws_scales, offs, offs2, offs3, offs4, offs5, offs6, offs7, out,
+):
+    nc = tc.nc
+    with ExitStack() as ctx:
+        sb = ctx.enter_context(tc.tile_pool(name="sb", bufs=1))
+        ps = ctx.enter_context(tc.psum_pool(name="ps", bufs=1))
+
+        def tile(name, shape, dtype, tag=None):
+            return sb.tile(shape, dtype, name=name, tag=tag or name, align_bytes=64)
+
+        def load_list(name, src):
+            lst = tile(name, list(src.shape), U16)
+            nc.sync.dma_start(lst[:], src)
+            return lst
+
+        def load_words(name, src, cols, dtype, tag=None):
+            words = tile(name, [P, cols], dtype, tag)
+            nc.sync.dma_start(words[:].bitcast(I32), src.bitcast(I32))
+            return words
+
+        def flat(words4):
+            return words4[0].rearrange("p n t -> p (n t)")
+
+        def load_plane(queue, plane, scales):
+            for q in range(QUADS):
+                queue.dma_start(
+                    plane[:].bitcast(I32)[32 * q : 32 * q + PACK, :],
+                    scales[0].bitcast(I32)[PACK * q : PACK * (q + 1), :],
+                )
+
+        def load_quadrant(queue, plane, scales, q):
+            rows = scales[0].bitcast(I32)[PACK * q : PACK * (q + 1), :]
+            queue.dma_start(
+                plane[:].bitcast(I32)[32 * q : 32 * (q + 1), :],
+                rows.unsqueeze(0).to_broadcast([32 // PACK, PACK, rows.shape[1]]),
+            )
+
+        def stage_rows(staged, scales):
+            nc.sync.dma_start(staged, scales[0].bitcast(I32).rearrange("(q r) n -> r q n", r=PACK))
+
+        def spread_rows(plane, staged):
+            for q in range(QUADS):
+                nc.vector.tensor_copy(plane[:].bitcast(I32)[32 * q : 32 * q + PACK, :], staged[:, q, :])
+
+        def gather(name, window, offsets, dtype, tag=None):
+            got = tile(name, [P, LANES * offsets.shape[1]], dtype, tag)
+            nc.vector.tensor_copy(got[:], window[:].indirect(offsets))
+            return got
+
+        def entries(lst, lo, hi):
+            return lst[:, lo // LANES : hi // LANES]
+
+        xt_plane = tile("xt_plane", [P, T], U8)
+        xo_plane = tile("xo_plane", [P, Z], U8)
+        w_staged = tile("w_staged", [PACK, QUADS, 3 * R // 4], I32)
+        xt_staged = tile("xt_staged", [PACK, QUADS, T // 4], I32)
+        w_plane = tile("w_plane", [P, 3 * R], U8)
+        wb_plane = tile("wb_plane", [P, N], U8)
+        ws_plane = tile("ws_plane", [P, N], U8)
+        for plane in (w_plane, xt_plane, ws_plane, wb_plane):
+            nc.vector.memset(plane[:].bitcast(I32), 0)
+        pages = [[tile("page%d_%d" % (c, i), [P, E], F32) for i in range(2)] for c in range(2)]
+        for c in range(2):
+            for i in range(2):
+                nc.gpsimd.memset(pages[c][i][:], 0.0)
+
+        for n, scales in enumerate((w_scales, w2_scales, w0_scales)):
+            stage_rows(w_staged[:, :, n * R // 4 : (n + 1) * R // 4], scales)
+        stage_rows(xt_staged[:], xt_scales)
+        idx = load_list("idx", offs)
+        xt_w = load_words("xt_w", xt_words[0], T, U16)
+        w_raw = load_words("w_raw", flat(w_words), R, U32)
+        xo_w = load_words("xo_w", flat(xo_words), Z, U32)
+        w2_raw = load_words("w2_raw", flat(w2_words), R, U32)
+        w0_raw = load_words("w0_raw", flat(w0_words), R, U32)
+        idx2 = load_list("idx2", offs2)
+        for q in range(QUADS):
+            load_quadrant(nc.sync, xo_plane, xo_scales, q)
+        idx5 = load_list("idx5", offs5)
+        idx3 = load_list("idx3", offs3)
+        idx4 = load_list("idx4", offs4)
+        ws_w = load_words("ws_w", flat(ws_words), N, U32)
+        wb_w = load_words("wb_w", wb_words[0], N, U16)
+        idx6 = load_list("idx6", offs6)
+        idx7 = load_list("idx7", offs7)
+        load_plane(nc.sync, ws_plane, ws_scales)
+        load_plane(nc.sync, wb_plane, wb_scales)
+
+        def deal_words(name, raw):
+            words = tile(name, [P, PACK, P], U32)
+            nc.scalar.copy(words[:].rearrange("p t m -> p m t"), raw[:].rearrange("p (m t) -> p m t", t=PACK))
+            return words
+
+        spread_rows(w_plane, w_staged)
+        w_s = tile("w_s", [P, PACK, P], U8)
+        nc.gpsimd.tensor_copy(w_s[:], w_plane[:, 0:R].rearrange("p (m t) -> p t m", t=PACK))
+        w_w = deal_words("w_w", w_raw)
+        spread_rows(xt_plane, xt_staged)
+        xt_s1 = gather("xt_s1", xt_plane, idx[:], U8)
+        xt_g1 = gather("xt_g1", xt_w, idx[:], U16)
+        b_s = tile("b_s", [P, 2, PACK, P], U8, "w_raw")
+        nc.vector.tensor_copy(b_s[:], w_plane[:, R : 3 * R].rearrange("p (n m t) -> p n t m", n=2, t=PACK))
+        w2_s, w0_s = b_s[:, 0], b_s[:, 1]
+        w2_w = deal_words("w2_w", w2_raw)
+        w0_w = deal_words("w0_w", w0_raw)
+        xo_g2 = gather("xo_g2", xo_w, idx2[:], U32)
+        xo_s2 = gather("xo_s2", xo_plane, idx2[:], U8)
+
+        a_ps = [ps.tile([P, 2, J], F32, name="a_ps%d" % i) for i in range(2)]
+        for t in range(PACK):
+            nc.tensor.matmul_mx(
+                a_ps[t // 2][:, t % 2, :], lhsT=w_w[:, t, :].bitcast(E4M3), lhsT_scale=w_s[:, t, :],
+                rhs=xt_g1[:].bitcast(E2M1), rhs_scale=xt_s1[:], start=True, stop=True,
+            )
+        a_sb = [tile("a_sb%d" % t, [P, J], F32) for t in range(PACK)]
+        for t in range(PACK):
+            nc.scalar.copy(a_sb[t][:], a_ps[t // 2][:, t % 2, :])
+        b_sb = [tile("b_sb%d" % t, [P, J], F32) for t in range(PACK)]
+        for t, bank in enumerate(("b_ps0", "a_ps0", "a_ps1", "b_ps0")):
+            b_ps = ps.tile([P, J], F32, name="b_ps%d" % t, tag=bank)
+            nc.tensor.matmul_mx(
+                b_ps[:], lhsT=w2_w[:, t, :].bitcast(E5M2), lhsT_scale=w2_s[:, t, :],
+                rhs=xt_g1[:].bitcast(E2M1), rhs_scale=xt_s1[:], start=True, stop=False,
+            )
+            nc.tensor.matmul_mx(
+                b_ps[:], lhsT=w0_w[:, t, :].bitcast(E5M2), lhsT_scale=w0_s[:, t, :],
+                rhs=xo_g2[:].bitcast(E4M3), rhs_scale=xo_s2[:], start=False, stop=True,
+            )
+            nc.vector.tensor_copy(b_sb[t][:], b_ps[:])
+
+        p_ps = [ps.tile([P, 2, HALF], F32, name="p_ps%d" % h) for h in range(2)]
+        picked = [tile("picked%d" % h, [P, PACK, HALF], BF16) for h in range(2)]
+        for h, (rows, lst, lean) in enumerate(((a_sb, idx3, b_sb), (b_sb, idx4, a_sb))):
+            for t in range(PACK):
+                nc.scalar.activation(picked[h][:, t, :], rows[t][:].indirect(lst[:]), COPY, scale=lean[t][:, 0:1])
+        xt_s5 = gather("xt_s5", xt_plane, idx5[:], U8, "xo_s2")
+        for h in range(2):
+            cols = slice(h * HALF, (h + 1) * HALF)
+            xt_g5 = gather("xt_g5_%d" % h, xt_w, entries(idx5, h * HALF, (h + 1) * HALF), U16, ("xo_g2", "woven")[h])
+            for i in range(2):
+                nc.tensor.matmul_mx(
+                    p_ps[h][:, i, :], lhsT=ws_w[:, i * P : (i + 1) * P].bitcast(E4M3),
+                    lhsT_scale=ws_plane[:, i * P : (i + 1) * P],
+                    rhs=xt_g5[:].bitcast(E2M1), rhs_scale=xt_s5[:, cols], start=(i == 0), stop=False,
+                )
+            woven = tile("woven%d" % h, [P, HALF, PACK], BF16, "woven")
+            nc.vector.tensor_copy(woven[:], picked[h][:].rearrange("p t d -> p d t"))
+            hid_w = tile("hid_w%d" % h, [P, HALF], U32)
+            hid_s = tile("hid_s%d" % h, [P, HALF], U8)
+            nc.vector.quantize_mx(hid_w[:].bitcast(E5M2), hid_s[:], woven[:].rearrange("p d t -> p (d t)"))
+            for i in range(2):
+                nc.tensor.matmul_mx(
+                    p_ps[h][:, i, :], lhsT=wb_w[:, i * P : (i + 1) * P].bitcast(E2M1),
+                    lhsT_scale=wb_plane[:, i * P : (i + 1) * P],
+                    rhs=hid_w[:].bitcast(E5M2), rhs_scale=hid_s[:], start=False, stop=(i == 1),
+                )
+            if h == 0:
+                early = [tile("early%d" % i, [P, HALF], F32) for i in range(2)]
+                for i in range(2):
+                    nc.scalar.copy(early[i][:], p_ps[0][:, i, :])
+
+        def put_scalar(c, lst, i, lo, hi, src):
+            nc.scalar.activation(pages[c][i][:].indirect(entries(lst, lo, hi)), src, COPY)
+
+        def put_vector(c, lst, i, lo, hi, src):
+            nc.vector.tensor_copy(pages[c][i][:].indirect(entries(lst, lo, hi)), src)
+
+        def finish(i, pieces, engine):
+            width = E // pieces
+            for j in range(pieces):
+                cols = slice(j * width, (j + 1) * width)
+                total = tile("total%d_%d" % (i, j), [P, width], F32)
+                engine.tensor_tensor(total[:], pages[0][i][:, cols], pages[1][i][:, cols], ADD)
+                nc.sync.dma_start(out[i * P : (i + 1) * P, cols], total[:])
+
+        QUART = HALF // 2
+        put_scalar(0, idx6, 0, 0, HALF, early[0][:])
+        put_vector(1, idx7, 0, 0, HALF, early[0][:])
+        put_scalar(1, idx7, 1, 0, QUART, early[1][:, 0:QUART])
+        put_scalar(0, idx6, 1, 0, HALF, early[1][:])
+        late = tile("late", [P, 2, HALF], F32, "early0")
+        nc.vector.tensor_copy(late[:], p_ps[1][:])
+        put_vector(1, idx7, 0, HALF, D, late[:, 0, :])
+        put_scalar(0, idx6, 0, HALF, D, late[:, 0, :])
+        put_vector(1, idx7, 1, QUART, HALF, early[1][:, QUART:HALF])
+        put_vector(1, idx7, 1, HALF, D, late[:, 1, :])
+        finish(0, 1, nc.gpsimd)
+        put_scalar(0, idx6, 1, HALF, D, late[:, 1, :])
+        finish(1, 2, nc.vector)

@@ -63,29 +63,24 @@ def tile_list_sidebyside_leaned_further_pagetwice_kernel(
                 rows.unsqueeze(0).to_broadcast([32 // PACK, PACK, rows.shape[1]]),
             )
 
-        def stage_rows(staged, scales):
-            nc.sync.dma_start(staged, scales[0].bitcast(I32).rearrange("(q r) n -> r q n", r=PACK))
+        def stage_rows(n, scales):
+            nc.sync.dma_start(
+                w_staged[:, :, n * R // 4 : (n + 1) * R // 4],
+                scales[0].bitcast(I32).rearrange("(q r) n -> r q n", r=PACK),
+            )
 
-        def spread_rows(plane, staged):
-            for q in range(QUADS):
-                nc.vector.tensor_copy(plane[:].bitcast(I32)[32 * q : 32 * q + PACK, :], staged[:, q, :])
-
-        def gather(name, window, offsets, dtype, tag=None):
-            got = tile(name, [P, LANES * offsets.shape[1]], dtype, tag)
-            nc.vector.tensor_copy(got[:], window[:].indirect(offsets))
+        def gather(name, window, lst, dtype, tag=None):
+            got = tile(name, [P, J], dtype, tag)
+            nc.vector.tensor_copy(got[:], window[:].indirect(lst[:]))
             return got
-
-        def entries(lst, lo, hi):
-            return lst[:, lo // LANES : hi // LANES]
 
         xt_plane = tile("xt_plane", [P, T], U8)
         xo_plane = tile("xo_plane", [P, Z], U8)
         w_staged = tile("w_staged", [PACK, QUADS, 3 * R // 4], I32)
-        xt_staged = tile("xt_staged", [PACK, QUADS, T // 4], I32)
         w_plane = tile("w_plane", [P, 3 * R], U8)
         wb_plane = tile("wb_plane", [P, N], U8)
         ws_plane = tile("ws_plane", [P, N], U8)
-        for plane in (w_plane, xt_plane, ws_plane, wb_plane):
+        for plane in (w_plane, ws_plane, wb_plane):
             nc.vector.memset(plane[:].bitcast(I32), 0)
         pages = [[tile("page%d_%d" % (c, i), [P, E], F32) for i in range(2)] for c in range(2)]
         for c in range(2):
@@ -93,14 +88,15 @@ def tile_list_sidebyside_leaned_further_pagetwice_kernel(
                 nc.gpsimd.memset(pages[c][i][:], 0.0)
 
         for n, scales in enumerate((w_scales, w2_scales, w0_scales)):
-            stage_rows(w_staged[:, :, n * R // 4 : (n + 1) * R // 4], scales)
-        stage_rows(xt_staged[:], xt_scales)
-        idx = load_list("idx", offs)
+            stage_rows(n, scales)
         xt_w = load_words("xt_w", xt_words[0], T, U16)
+        idx = load_list("idx", offs)
         w_raw = load_words("w_raw", flat(w_words), R, U32)
-        xo_w = load_words("xo_w", flat(xo_words), Z, U32)
+        for q in range(QUADS):
+            load_quadrant(nc.sync, xt_plane, xt_scales, q)
         w2_raw = load_words("w2_raw", flat(w2_words), R, U32)
         w0_raw = load_words("w0_raw", flat(w0_words), R, U32)
+        xo_w = load_words("xo_w", flat(xo_words), Z, U32)
         idx2 = load_list("idx2", offs2)
         for q in range(QUADS):
             load_quadrant(nc.sync, xo_plane, xo_scales, q)
@@ -114,64 +110,67 @@ def tile_list_sidebyside_leaned_further_pagetwice_kernel(
         load_plane(nc.sync, ws_plane, ws_scales)
         load_plane(nc.sync, wb_plane, wb_scales)
 
-        def deal_words(name, raw):
-            words = tile(name, [P, PACK, P], U32)
+        def deal(name, raw, n, engine):
+            words = tile(name + "_w", [P, PACK, P], U32)
             nc.scalar.copy(words[:].rearrange("p t m -> p m t"), raw[:].rearrange("p (m t) -> p m t", t=PACK))
-            return words
+            plane = tile(name + "_s", [P, PACK, P], U8)
+            engine.tensor_copy(
+                plane[:], w_plane[:, n * R : (n + 1) * R].rearrange("p (m t) -> p t m", t=PACK),
+            )
+            return words, plane
 
-        spread_rows(w_plane, w_staged)
-        w_s = tile("w_s", [P, PACK, P], U8)
-        nc.gpsimd.tensor_copy(w_s[:], w_plane[:, 0:R].rearrange("p (m t) -> p t m", t=PACK))
-        w_w = deal_words("w_w", w_raw)
-        spread_rows(xt_plane, xt_staged)
-        xt_s1 = gather("xt_s1", xt_plane, idx[:], U8)
-        xt_g1 = gather("xt_g1", xt_w, idx[:], U16)
-        b_s = tile("b_s", [P, 2, PACK, P], U8, "w_raw")
-        nc.vector.tensor_copy(b_s[:], w_plane[:, R : 3 * R].rearrange("p (n m t) -> p n t m", n=2, t=PACK))
-        w2_s, w0_s = b_s[:, 0], b_s[:, 1]
-        w2_w = deal_words("w2_w", w2_raw)
-        w0_w = deal_words("w0_w", w0_raw)
-        xo_g2 = gather("xo_g2", xo_w, idx2[:], U32)
-        xo_s2 = gather("xo_s2", xo_plane, idx2[:], U8)
+        for q in range(QUADS):
+            nc.vector.tensor_copy(w_plane[:].bitcast(I32)[32 * q : 32 * q + PACK, :], w_staged[:, q, :])
+        w_w, w_s = deal("w", w_raw, 0, nc.vector)
+        xt_g1 = gather("xt_g1", xt_w, idx, U16)
+        xt_s1 = gather("xt_s1", xt_plane, idx, U8)
+        w2_w, w2_s = deal("w2", w2_raw, 1, nc.vector)
+        w0_w, w0_s = deal("w0", w0_raw, 2, nc.vector)
+        xo_g2 = gather("xo_g2", xo_w, idx2, U32)
+        xo_s2 = gather("xo_s2", xo_plane, idx2, U8)
 
         a_ps = [ps.tile([P, 2, J], F32, name="a_ps%d" % i) for i in range(2)]
+        b_ps = [ps.tile([P, J], F32, name="b_ps%d" % t) for t in range(PACK)]
         for t in range(PACK):
             nc.tensor.matmul_mx(
                 a_ps[t // 2][:, t % 2, :], lhsT=w_w[:, t, :].bitcast(E4M3), lhsT_scale=w_s[:, t, :],
                 rhs=xt_g1[:].bitcast(E2M1), rhs_scale=xt_s1[:], start=True, stop=True,
             )
+        for t in range(PACK):
+            nc.tensor.matmul_mx(
+                b_ps[t][:], lhsT=w2_w[:, t, :].bitcast(E5M2), lhsT_scale=w2_s[:, t, :],
+                rhs=xt_g1[:].bitcast(E2M1), rhs_scale=xt_s1[:], start=True, stop=False,
+            )
         a_sb = [tile("a_sb%d" % t, [P, J], F32) for t in range(PACK)]
         for t in range(PACK):
             nc.scalar.copy(a_sb[t][:], a_ps[t // 2][:, t % 2, :])
-        b_sb = [tile("b_sb%d" % t, [P, J], F32) for t in range(PACK)]
-        for t, bank in enumerate(("b_ps0", "a_ps0", "a_ps1", "b_ps0")):
-            b_ps = ps.tile([P, J], F32, name="b_ps%d" % t, tag=bank)
+        for t in range(PACK):
             nc.tensor.matmul_mx(
-                b_ps[:], lhsT=w2_w[:, t, :].bitcast(E5M2), lhsT_scale=w2_s[:, t, :],
-                rhs=xt_g1[:].bitcast(E2M1), rhs_scale=xt_s1[:], start=True, stop=False,
-            )
-            nc.tensor.matmul_mx(
-                b_ps[:], lhsT=w0_w[:, t, :].bitcast(E5M2), lhsT_scale=w0_s[:, t, :],
+                b_ps[t][:], lhsT=w0_w[:, t, :].bitcast(E5M2), lhsT_scale=w0_s[:, t, :],
                 rhs=xo_g2[:].bitcast(E4M3), rhs_scale=xo_s2[:], start=False, stop=True,
             )
-            nc.vector.tensor_copy(b_sb[t][:], b_ps[:])
+        xt_s5 = gather("xt_s5", xt_plane, idx5, U8)
+        b_sb = [tile("b_sb%d" % t, [P, J], F32) for t in range(PACK)]
+        for t in range(PACK):
+            nc.vector.tensor_copy(b_sb[t][:], b_ps[t][:])
+        xt_g5 = gather("xt_g5", xt_w, idx5, U16, "xo_g2")
 
         p_ps = [ps.tile([P, 2, HALF], F32, name="p_ps%d" % h) for h in range(2)]
+        looks = ((a_sb, idx3, b_sb), (b_sb, idx4, a_sb))
         picked = [tile("picked%d" % h, [P, PACK, HALF], BF16) for h in range(2)]
-        for h, (rows, lst, lean) in enumerate(((a_sb, idx3, b_sb), (b_sb, idx4, a_sb))):
+        for h, (rows, lst, lean) in enumerate(looks):
             for t in range(PACK):
                 nc.scalar.activation(picked[h][:, t, :], rows[t][:].indirect(lst[:]), COPY, scale=lean[t][:, 0:1])
-        xt_s5 = gather("xt_s5", xt_plane, idx5[:], U8, "xo_s2")
         for h in range(2):
             cols = slice(h * HALF, (h + 1) * HALF)
-            xt_g5 = gather("xt_g5_%d" % h, xt_w, entries(idx5, h * HALF, (h + 1) * HALF), U16, ("xo_g2", "woven")[h])
             for i in range(2):
                 nc.tensor.matmul_mx(
                     p_ps[h][:, i, :], lhsT=ws_w[:, i * P : (i + 1) * P].bitcast(E4M3),
                     lhsT_scale=ws_plane[:, i * P : (i + 1) * P],
-                    rhs=xt_g5[:].bitcast(E2M1), rhs_scale=xt_s5[:, cols], start=(i == 0), stop=False,
+                    rhs=xt_g5[:, cols].bitcast(E2M1), rhs_scale=xt_s5[:, cols], start=(i == 0), stop=False,
                 )
-            woven = tile("woven%d" % h, [P, HALF, PACK], BF16, "woven")
+        for h in range(2):
+            woven = tile("woven", [P, HALF, PACK], BF16)
             nc.vector.tensor_copy(woven[:], picked[h][:].rearrange("p t d -> p d t"))
             hid_w = tile("hid_w%d" % h, [P, HALF], U32)
             hid_s = tile("hid_s%d" % h, [P, HALF], U8)
@@ -187,6 +186,9 @@ def tile_list_sidebyside_leaned_further_pagetwice_kernel(
                 for i in range(2):
                     nc.scalar.copy(early[i][:], p_ps[0][:, i, :])
 
+        def entries(lst, lo, hi):
+            return lst[:, lo // LANES : hi // LANES]
+
         def put_scalar(c, lst, i, lo, hi, src):
             nc.scalar.activation(pages[c][i][:].indirect(entries(lst, lo, hi)), src, COPY)
 
@@ -201,17 +203,15 @@ def tile_list_sidebyside_leaned_further_pagetwice_kernel(
                 engine.tensor_tensor(total[:], pages[0][i][:, cols], pages[1][i][:, cols], ADD)
                 nc.sync.dma_start(out[i * P : (i + 1) * P, cols], total[:])
 
-        QUART = HALF // 2
         put_scalar(0, idx6, 0, 0, HALF, early[0][:])
         put_vector(1, idx7, 0, 0, HALF, early[0][:])
-        put_scalar(1, idx7, 1, 0, QUART, early[1][:, 0:QUART])
+        put_scalar(1, idx7, 1, 0, HALF, early[1][:])
         put_scalar(0, idx6, 1, 0, HALF, early[1][:])
         late = tile("late", [P, 2, HALF], F32, "early0")
         nc.vector.tensor_copy(late[:], p_ps[1][:])
         put_vector(1, idx7, 0, HALF, D, late[:, 0, :])
         put_scalar(0, idx6, 0, HALF, D, late[:, 0, :])
-        put_vector(1, idx7, 1, QUART, HALF, early[1][:, QUART:HALF])
         put_vector(1, idx7, 1, HALF, D, late[:, 1, :])
-        finish(0, 1, nc.gpsimd)
+        finish(0, 1, nc.vector)
         put_scalar(0, idx6, 1, HALF, D, late[:, 1, :])
         finish(1, 2, nc.vector)

@@ -85,7 +85,7 @@ def tile_list_sidebyside_leaned_further_pagetwice_kernel(
         pages = [[tile("page%d_%d" % (c, i), [P, E], F32) for i in range(2)] for c in range(2)]
         for c in range(2):
             for i in range(2):
-                nc.gpsimd.memset(pages[c][i][:], 0.0)
+                nc.vector.memset(pages[c][i][:], 0.0)
 
         for n, scales in enumerate((w_scales, w2_scales, w0_scales)):
             stage_rows(n, scales)

from contextlib import ExitStack

import concourse.mybir as mybir

K, T, J, R, F, Z, O, U, D, N, E = 512, 1024, 256, 512, 512, 1024, 128, 128, 256, 256, 512
FLOPS = 2 * (3 * K * R * J + 2 * R * N * D)

F32 = mybir.dt.float32
BF16 = mybir.dt.bfloat16
I32 = mybir.dt.int32
U32 = mybir.dt.uint32
U16 = mybir.dt.uint16
U8 = mybir.dt.uint8
E4M3 = mybir.dt.float8_e4m3fn_x4
E5M2 = mybir.dt.float8_e5m2_x4
E2M1 = mybir.dt.float4_e2m1fn_x4
COPY = mybir.ActivationFunctionType.Copy
ADD = mybir.AluOpType.add

P = 128
PACK = 4
QUADS = 4
LANES = 16
HALF = D // 2


def tile_list_sidebyside_leaned_further_pagetwice_kernel(
    tc, xt_words, xt_scales, xo_words, xo_scales, w_words, w_scales, w2_words, w2_scales, w0_words, w0_scales,
    wb_words, wb_scales, ws_words, ws_scales, offs, offs2, offs3, offs4, offs5, offs6, offs7, out,
):
    nc = tc.nc
    with ExitStack() as ctx:
        sb = ctx.enter_context(tc.tile_pool(name="sb", bufs=1))
        ps = ctx.enter_context(tc.psum_pool(name="ps", bufs=1))

        def tile(name, shape, dtype, tag=None):
            return sb.tile(shape, dtype, name=name, tag=tag or name, align_bytes=64)

        def load_list(name, src):
            lst = tile(name, list(src.shape), U16)
            nc.sync.dma_start(lst[:], src)
            return lst

        def load_words(name, src, cols, dtype, tag=None):
            words = tile(name, [P, cols], dtype, tag)
            nc.sync.dma_start(words[:].bitcast(I32), src.bitcast(I32))
            return words

        def flat(words4):
            return words4[0].rearrange("p n t -> p (n t)")

        def load_plane(queue, plane, scales):
            for q in range(QUADS):
                queue.dma_start(
                    plane[:].bitcast(I32)[32 * q : 32 * q + PACK, :],
                    scales[0].bitcast(I32)[PACK * q : PACK * (q + 1), :],
                )

        def load_quadrant(queue, plane, scales, q):
            rows = scales[0].bitcast(I32)[PACK * q : PACK * (q + 1), :]
            queue.dma_start(
                plane[:].bitcast(I32)[32 * q : 32 * (q + 1), :],
                rows.unsqueeze(0).to_broadcast([32 // PACK, PACK, rows.shape[1]]),
            )

        def stage_rows(n, scales):
            nc.sync.dma_start(
                w_staged[:, :, n * R // 4 : (n + 1) * R // 4],
                scales[0].bitcast(I32).rearrange("(q r) n -> r q n", r=PACK),
            )

        def gather(name, window, lst, dtype, tag=None):
            got = tile(name, [P, J], dtype, tag)
            nc.vector.tensor_copy(got[:], window[:].indirect(lst[:]))
            return got

        xt_plane = tile("xt_plane", [P, T], U8)
        xo_plane = tile("xo_plane", [P, Z], U8)
        w_staged = tile("w_staged", [PACK, QUADS, 3 * R // 4], I32)
        w_plane = tile("w_plane", [P, 3 * R], U8)
        wb_plane = tile("wb_plane", [P, N], U8)
        ws_plane = tile("ws_plane", [P, N], U8)
        for plane in (w_plane, ws_plane, wb_plane):
            nc.vector.memset(plane[:].bitcast(I32), 0)
        pages = [[tile("page%d_%d" % (c, i), [P, E], F32) for i in range(2)] for c in range(2)]
        for c in range(2):
            for i in range(2):
                nc.vector.memset(pages[c][i][:], 0.0)

        for n, scales in enumerate((w_scales, w2_scales, w0_scales)):
            stage_rows(n, scales)
        xt_w = load_words("xt_w", xt_words[0], T, U16)
        idx = load_list("idx", offs)
        w_raw = load_words("w_raw", flat(w_words), R, U32)
        for q in range(QUADS):
            load_quadrant(nc.sync, xt_plane, xt_scales, q)
        w2_raw = load_words("w2_raw", flat(w2_words), R, U32)
        w0_raw = load_words("w0_raw", flat(w0_words), R, U32)
        xo_w = load_words("xo_w", flat(xo_words), Z, U32)
        idx2 = load_list("idx2", offs2)
        for q in range(QUADS):
            load_quadrant(nc.sync, xo_plane, xo_scales, q)
        idx5 = load_list("idx5", offs5)
        idx3 = load_list("idx3", offs3)
        idx4 = load_list("idx4", offs4)
        ws_w = load_words("ws_w", flat(ws_words), N, U32)
        wb_w = load_words("wb_w", wb_words[0], N, U16)
        idx6 = load_list("idx6", offs6)
        idx7 = load_list("idx7", offs7)
        load_plane(nc.sync, ws_plane, ws_scales)
        load_plane(nc.sync, wb_plane, wb_scales)

        def deal(name, raw, n, engine):
            words = tile(name + "_w", [P, PACK, P], U32)
            nc.scalar.copy(words[:].rearrange("p t m -> p m t"), raw[:].rearrange("p (m t) -> p m t", t=PACK))
            plane = tile(name + "_s", [P, PACK, P], U8)
            engine.tensor_copy(
                plane[:], w_plane[:, n * R : (n + 1) * R].rearrange("p (m t) -> p t m", t=PACK),
            )
            return words, plane

        for q in range(QUADS):
            nc.vector.tensor_copy(w_plane[:].bitcast(I32)[32 * q : 32 * q + PACK, :], w_staged[:, q, :])
        w_w, w_s = deal("w", w_raw, 0, nc.vector)
        xt_g1 = gather("xt_g1", xt_w, idx, U16)
        xt_s1 = gather("xt_s1", xt_plane, idx, U8)
        w2_w, w2_s = deal("w2", w2_raw, 1, nc.vector)
        w0_w, w0_s = deal("w0", w0_raw, 2, nc.vector)
        xo_g2 = gather("xo_g2", xo_w, idx2, U32)
        xo_s2 = gather("xo_s2", xo_plane, idx2, U8)

        a_ps = [ps.tile([P, 2, J], F32, name="a_ps%d" % i) for i in range(2)]
        b_ps = [ps.tile([P, J], F32, name="b_ps%d" % t) for t in range(PACK)]
        for t in range(PACK):
            nc.tensor.matmul_mx(
                a_ps[t // 2][:, t % 2, :], lhsT=w_w[:, t, :].bitcast(E4M3), lhsT_scale=w_s[:, t, :],
                rhs=xt_g1[:].bitcast(E2M1), rhs_scale=xt_s1[:], start=True, stop=True,
            )
        for t in range(PACK):
            nc.tensor.matmul_mx(
                b_ps[t][:], lhsT=w2_w[:, t, :].bitcast(E5M2), lhsT_scale=w2_s[:, t, :],
                rhs=xt_g1[:].bitcast(E2M1), rhs_scale=xt_s1[:], start=True, stop=False,
            )
        a_sb = [tile("a_sb%d" % t, [P, J], F32) for t in range(PACK)]
        for t in range(PACK):
            nc.scalar.copy(a_sb[t][:], a_ps[t // 2][:, t % 2, :])
        for t in range(PACK):
            nc.tensor.matmul_mx(
                b_ps[t][:], lhsT=w0_w[:, t, :].bitcast(E5M2), lhsT_scale=w0_s[:, t, :],
                rhs=xo_g2[:].bitcast(E4M3), rhs_scale=xo_s2[:], start=False, stop=True,
            )
        xt_s5 = gather("xt_s5", xt_plane, idx5, U8)
        b_sb = [tile("b_sb%d" % t, [P, J], F32) for t in range(PACK)]
        for t in range(PACK):
            nc.vector.tensor_copy(b_sb[t][:], b_ps[t][:])
        xt_g5 = gather("xt_g5", xt_w, idx5, U16, "xo_g2")

        p_ps = [ps.tile([P, 2, HALF], F32, name="p_ps%d" % h) for h in range(2)]
        looks = ((a_sb, idx3, b_sb), (b_sb, idx4, a_sb))
        picked = [tile("picked%d" % h, [P, PACK, HALF], BF16) for h in range(2)]
        for h, (rows, lst, lean) in enumerate(looks):
            for t in range(PACK):
                nc.scalar.activation(picked[h][:, t, :], rows[t][:].indirect(lst[:]), COPY, scale=lean[t][:, 0:1])
        for h in range(2):
            cols = slice(h * HALF, (h + 1) * HALF)
            for i in range(2):
                nc.tensor.matmul_mx(
                    p_ps[h][:, i, :], lhsT=ws_w[:, i * P : (i + 1) * P].bitcast(E4M3),
                    lhsT_scale=ws_plane[:, i * P : (i + 1) * P],
                    rhs=xt_g5[:, cols].bitcast(E2M1), rhs_scale=xt_s5[:, cols], start=(i == 0), stop=False,
                )
        for h in range(2):
            woven = tile("woven", [P, HALF, PACK], BF16)
            nc.vector.tensor_copy(woven[:], picked[h][:].rearrange("p t d -> p d t"))
            hid_w = tile("hid_w%d" % h, [P, HALF], U32)
            hid_s = tile("hid_s%d" % h, [P, HALF], U8)
            nc.vector.quantize_mx(hid_w[:].bitcast(E5M2), hid_s[:], woven[:].rearrange("p d t -> p (d t)"))
            for i in range(2):
                nc.tensor.matmul_mx(
                    p_ps[h][:, i, :], lhsT=wb_w[:, i * P : (i + 1) * P].bitcast(E2M1),
                    lhsT_scale=wb_plane[:, i * P : (i + 1) * P],
                    rhs=hid_w[:].bitcast(E5M2), rhs_scale=hid_s[:], start=False, stop=(i == 1),
                )
            if h == 0:
                early = [tile("early%d" % i, [P, HALF], F32) for i in range(2)]
                for i in range(2):
                    nc.scalar.copy(early[i][:], p_ps[0][:, i, :])

        def entries(lst, lo, hi):
            return lst[:, lo // LANES : hi // LANES]

        def put_scalar(c, lst, i, lo, hi, src):
            nc.scalar.activation(pages[c][i][:].indirect(entries(lst, lo, hi)), src, COPY)

        def put_vector(c, lst, i, lo, hi, src):
            nc.vector.tensor_copy(pages[c][i][:].indirect(entries(lst, lo, hi)), src)

        def finish(i, pieces, engine):
            width = E // pieces
            for j in range(pieces):
                cols = slice(j * width, (j + 1) * width)
                total = tile("total%d_%d" % (i, j), [P, width], F32)
                engine.tensor_tensor(total[:], pages[0][i][:, cols], pages[1][i][:, cols], ADD)
                nc.sync.dma_start(out[i * P : (i + 1) * P, cols], total[:])

        put_scalar(0, idx6, 0, 0, HALF, early[0][:])
        put_vector(1, idx7, 0, 0, HALF, early[0][:])
        put_scalar(1, idx7, 1, 0, HALF, early[1][:])
        put_scalar(0, idx6, 1, 0, HALF, early[1][:])
        late = tile("late", [P, 2, HALF], F32, "early0")
        nc.vector.tensor_copy(late[:], p_ps[1][:])
        put_vector(1, idx7, 0, HALF, D, late[:, 0, :])
        put_scalar(0, idx6, 0, HALF, D, late[:, 0, :])
        put_vector(1, idx7, 1, HALF, D, late[:, 1, :])
        finish(0, 1, nc.vector)
        put_scalar(0, idx6, 1, HALF, D, late[:, 1, :])
        finish(1, 2, nc.vector)
